import numpy as np
import ml_dtypes


def mxq(x, axis, fmt="e4m3"):
    dtype, down = {"e4m3": (ml_dtypes.float8_e4m3fn, 7), "e5m2": (ml_dtypes.float8_e5m2, 14)}[fmt]
    v = np.moveaxis(np.asarray(x, np.float32).astype(ml_dtypes.bfloat16).astype(np.float64), axis, -1)
    blocks = v.reshape(v.shape[:-1] + (-1, 32))
    amax = np.abs(blocks).max(-1, keepdims=True)
    byte = np.maximum(np.where(amax > 0, np.frexp(amax)[1] - 1 + 127, 0) - down, 1)
    scale = np.exp2(byte - 127.0)
    codes = (blocks / scale).astype(np.float32).astype(dtype).astype(np.float64)
    return np.moveaxis((codes * scale).reshape(v.shape), -1, axis)


WIDE = False


def mx_kscale(k):
    if not WIDE:
        return np.ones(k)
    levels = np.array([10, -10, 5, -5, 0])
    if k % 512:
        return np.exp2(np.random.permutation(np.resize(levels, k // 32))).repeat(32)
    a = np.empty((k // 512, 16))
    for p in range(k // 512):
        a[p, :8] = np.random.permutation(np.resize(levels, 8))
        for g in range(8):
            far = levels[np.abs(levels - a[p, g]) >= 10]
            a[p, g + 8] = far[np.random.randint(len(far))]
    return np.exp2(a.ravel()).repeat(32)


def f64(x):
    return np.asarray(x).astype(np.float64)


def striped(idx):
    return np.tile(np.asarray(idx).reshape(-1, 16).T, (8, 1)).astype(np.uint16)


def unstriped(offs):
    return offs[:16].T.reshape(-1).astype(np.int64)


B, N, T, D, DV, NQ = 1, 1024, 4096, 512, 512, 128


def setup_inputs():
    n = np.random.standard_normal
    idx = np.sort(np.random.permutation(T)[:B * N].reshape(B, N), axis=1).reshape(-1)
    s = mx_kscale(D)[:, None]
    u = np.ones(T)
    u[idx] = mx_kscale(B * N)
    r = np.random.uniform(0.5, 2.0, T)
    raw = n((D, T)) / s / (u * r)
    when = np.zeros(T)
    when[idx] = np.sort(np.random.permutation(2 * N)[:B * N])
    return {
        "qT": (n((B, D, NQ)) * s * (0.80 / np.sqrt(D))).astype(np.float32),
        "cT": raw.astype(np.float32),
        "ts": np.tile(u * r, (128, 1)).astype(np.float32),
        "pos": np.tile(when, (128, 1)).astype(np.float32),
        "slope": np.exp2(-np.random.randint(8, 13, (B, NQ, 1))).astype(np.float32),
        "ch": np.tile(s[:, 0] * np.random.uniform(0.5, 2.0, D), (128, 1)).astype(np.float32),
        "offs": striped(idx),
    }


def reference(qT, cT, ts, pos, slope, ch, offs):
    idx = unstriped(offs)
    c = f64(cT)
    pick = lambda x: x[:, idx].reshape(x.shape[0], B, N).transpose(1, 0, 2)
    q = f64(qT)
    score = mxq(q, 1, "e4m3").transpose(0, 2, 1) @ mxq(pick(c), 1, "e4m3")
    score = score * pick(f64(ts))[:, :1, :]
    score = score + f64(slope) * pick(f64(pos))[:, :1, :]
    m = score.max(-1, keepdims=True)
    p = np.exp(score - m)
    total = p.sum(-1, keepdims=True)
    w = p * pick(f64(ts))[:, :1, :]
    y = mxq(w, 2, "e4m3") @ mxq(pick(c).transpose(0, 2, 1), 1, "e4m3")
    y = y / total
    y = y * f64(ch)[:1]
    return y

@@ -1,0 +1,241 @@
+from contextlib import ExitStack
+
+import concourse.mybir as mybir
+from concourse.masks import make_identity
+
+NQ, N, T, D = 128, 1024, 4096, 512
+P = 128
+PACK = 4
+HALF = 512
+
+F32 = mybir.dt.float32
+BF16 = mybir.dt.bfloat16
+U32 = mybir.dt.uint32
+U16 = mybir.dt.uint16
+U8 = mybir.dt.uint8
+FP8X4 = mybir.dt.float8_e4m3fn_x4
+ACT = mybir.ActivationFunctionType
+ALU = mybir.AluOpType
+AX = mybir.AxisListType
+
+FLOPS = 2 * 2 * NQ * N * D
+BYTES = 4 * (D * T + D * NQ + 2 * T + NQ + D + NQ * D) + 2 * P * N // 16
+
+
+def tile_attend_x_mla_alibi_srt_kernel(tc, qT, cT, ts, pos, slope, ch, offs, out):
+    nc = tc.nc
+    with ExitStack() as ctx:
+        keep = ctx.enter_context(tc.tile_pool(name="keep", bufs=1))
+        psum_tr = ctx.enter_context(tc.psum_pool(name="psum_tr", bufs=2))
+        psum_v = ctx.enter_context(tc.psum_pool(name="psum_v", bufs=2))
+        psum_s = ctx.enter_context(tc.psum_pool(name="psum_s", bufs=1))
+
+        offsets = keep.tile([P, N // 16], U16, name="offsets")
+        nc.sync.dma_start(offsets[:], offs)
+
+        planes = []
+        for t in range(PACK):
+            plane = keep.tile([P, T], F32, name=f"plane{t}")
+            planes.append(plane)
+        tsw = keep.tile([P, T], F32, name="tsw")
+        posw = keep.tile([P, T], F32, name="posw")
+        slope_sb = keep.tile([P, 1], F32, name="slope_sb")
+        q_raw = keep.tile([P, PACK, NQ], F32, name="q_raw")
+        ch_sb = keep.tile([P, D], F32, name="ch_sb")
+
+        c_view = cT.rearrange("(p t) n -> t p n", t=PACK)
+        nc.sync.dma_start(out=planes[0][:], in_=c_view[0])
+        ident_f = keep.tile([P, P], F32, name="ident_f")
+        make_identity(nc, ident_f[:])
+        ident_b = keep.tile([P, P], BF16, name="ident_b")
+        make_identity(nc, ident_b[:])
+        nc.scalar.dma_start(out=slope_sb[:], in_=slope[0])
+        for window, held in ((tsw, (planes[1],)), (posw, (planes[2], planes[3], ch_sb))):
+            nc.vector.memset(window[:, 0 : T // 2], 0.0)
+            nc.gpsimd.memset(window[:, T // 2 : T], 0.0)
+            for late in held:
+                nc.vector.memset(late[:, 0:8], 0.0)
+                nc.gpsimd.memset(late[:, 8:16], 0.0)
+        nc.vector.memset(q_raw[:, 0, 0:8], 0.0)
+        nc.sync.dma_start(out=tsw[0:1, :], in_=ts[0:1, :])
+        nc.sync.dma_start(out=planes[1][:], in_=c_view[1])
+        nc.sync.dma_start(out=posw[0:1, :], in_=pos[0:1, :])
+        nc.sync.dma_start(out=planes[2][:], in_=c_view[2])
+        nc.sync.dma_start(out=planes[3][:], in_=c_view[3])
+        nc.sync.dma_start(out=q_raw[:], in_=qT[0].rearrange("(p t) q -> p t q", t=PACK))
+        nc.sync.dma_start(out=ch_sb[:], in_=ch)
+
+
+        warm = keep.tile([P, 1], F32, name="warm")
+        nc.gpsimd.memset(warm[:], 0.0)
+        nc.scalar.activation(warm[:], warm[:], ACT.Exp)
+
+        def pick(window, label):
+            picked = keep.tile([P, N], F32, name=f"{label}_picked")
+            nc.vector.tensor_copy(picked[:], window[:].indirect(offsets[:]))
+            return picked
+
+        def spread(picked, label):
+            cols = keep.tile([P, 2, PACK], F32, name=f"{label}_cols")
+            for g in range(2):
+                turned = psum_tr.tile([P, PACK, P], F32, name="turn")
+                for t in range(PACK):
+                    nc.tensor.transpose(turned[:, t, :], picked[:, HALF * g + t : HALF * (g + 1) : PACK], ident_f[:])
+                nc.scalar.copy(cols[:, g, :], turned[:, :, 0])
+            rows = []
+            for g in range(2):
+                wide = psum_tr.tile([P, PACK, P], F32, name="turn")
+                for t in range(PACK):
+                    nc.tensor.transpose(wide[:, t, :], cols[:, g, t : t + 1].to_broadcast([P, P]), ident_f[:])
+                rows.append(wide)
+            return cols, rows
+
+        latents = keep.tile([P, N, PACK], BF16, name="latents", align_bytes=64)
+        val_codes = keep.tile([P, 2, PACK, P], U32, name="val_codes", align_bytes=64)
+        val_scales = keep.tile([P, 2, PACK, P], U8, name="val_scales", align_bytes=64)
+
+        def gather(t, g):
+            cols = slice(HALF * g, HALF * (g + 1))
+            nc.vector.tensor_copy(latents[:, cols, t], planes[t][:].indirect(offsets[:, 32 * g : 32 * (g + 1)]))
+
+        def gather_whole(t):
+            nc.vector.tensor_copy(latents[:, :, t], planes[t][:].indirect(offsets[:]))
+
+        val_grouped = {}
+
+        def turn_values(t):
+            for g in range(2):
+                turned = psum_v.tile([P, PACK, P], BF16, name="turn_v")
+                for j in range(PACK):
+                    nc.tensor.transpose(turned[:, j, :], latents[:, HALF * g + j : HALF * (g + 1) : PACK, t], ident_b[:])
+                grouped = keep.tile([P, P, PACK], BF16, name=f"val{t}_{g}", align_bytes=64)
+                nc.scalar.copy(grouped[:], turned[:].rearrange("s j e -> s e j"))
+                val_grouped[t, g] = grouped
+
+        def quantize_values(t):
+            for g in range(2):
+                nc.vector.quantize_mx(
+                    out=val_codes[:, g, t, :].bitcast(FP8X4),
+                    scales=val_scales[:, g, t, :],
+                    in_=val_grouped[t, g][:].rearrange("s e j -> s (e j)"),
+                )
+
+        ts_picked = pick(tsw, "ts")
+        gather_whole(0)
+        turn_values(0)
+        ts_cols, rows = spread(ts_picked, "ts")
+        ts_rows = keep.tile([P, 2, P, PACK], F32, name="ts_rows")
+        for g in range(2):
+            nc.scalar.copy(ts_rows[:, g], rows[g][:].rearrange("q t i -> q i t"))
+
+        gather_whole(1)
+        turn_values(1)
+        pos_picked = pick(posw, "pos")
+        pos_cols, rows = spread(pos_picked, "pos")
+        bias = keep.tile([P, 2, P, PACK], F32, name="bias")
+        for g in range(2):
+            nc.scalar.activation(bias[:, g], rows[g][:].rearrange("q t i -> q i t"), ACT.Copy, scale=slope_sb[:])
+
+        quantize_values(0)
+        gather_whole(2)
+        quantize_values(1)
+
+        key_codes = keep.tile([P, 2, HALF], U32, name="key_codes", align_bytes=64)
+        key_scales = keep.tile([P, 2, HALF], U8, name="key_scales", align_bytes=64)
+        q_grouped = keep.tile([P, NQ, PACK], BF16, name="q_grouped", align_bytes=64)
+        q_codes = keep.tile([P, NQ], U32, name="q_codes", align_bytes=64)
+        q_scales = keep.tile([P, NQ], U8, name="q_scales", align_bytes=64)
+        nc.scalar.copy(q_grouped[:], q_raw[:].rearrange("p t q -> p q t"))
+
+        scores = []
+        for g in range(2):
+            gather(3, g)
+            if g == 0:
+                nc.vector.quantize_mx(
+                    out=q_codes[:].bitcast(FP8X4), scales=q_scales[:], in_=q_grouped[:].rearrange("p q t -> p (q t)")
+                )
+            nc.vector.quantize_mx(
+                out=key_codes[:, g, :].bitcast(FP8X4),
+                scales=key_scales[:, g, :],
+                in_=latents[:, HALF * g : HALF * (g + 1), :].rearrange("p i t -> p (i t)"),
+            )
+            acc = psum_s.tile([NQ, HALF], F32, name=f"scores{g}")
+            nc.tensor.matmul_mx(
+                out=acc[:],
+                lhsT=q_codes[:].bitcast(FP8X4),
+                lhsT_scale=q_scales[:],
+                rhs=key_codes[:, g, :].bitcast(FP8X4),
+                rhs_scale=key_scales[:, g, :],
+                start=True,
+                stop=True,
+            )
+            scores.append(acc)
+
+        turn_values(2)
+        turn_values(3)
+
+        scaled = keep.tile([P, 2, HALF], F32, name="scaled")
+        biased = keep.tile([P, 2, HALF], F32, name="biased")
+        peaks = keep.tile([P, 2], F32, name="peaks")
+        for g in range(2):
+            nc.vector.tensor_tensor(scaled[:, g, :], scores[g][:], ts_rows[:, g].rearrange("q i t -> q (i t)"), ALU.mult)
+            nc.vector.tensor_tensor(biased[:, g, :], scaled[:, g, :], bias[:, g].rearrange("q i t -> q (i t)"), ALU.add)
+            nc.vector.reduce_max(peaks[:, g : g + 1], biased[:, g, :], axis=AX.X)
+        minus_peak = keep.tile([P, 1], F32, name="minus_peak")
+        nc.vector.tensor_scalar(minus_peak[:], peaks[:, 0:1], peaks[:, 1:2], -1.0, ALU.max, ALU.mult)
+
+        quantize_values(2)
+        quantize_values(3)
+
+        probs = keep.tile([P, 2, PACK, P], F32, name="probs")
+        sums = keep.tile([P, 2], F32, name="sums")
+        for g in range(2):
+            nc.scalar.activation(
+                probs[:, g].rearrange("q t i -> q i t"),
+                biased[:, g, :].rearrange("q (i t) -> q i t", t=PACK),
+                ACT.Exp,
+                bias=minus_peak[:],
+                accum_out=sums[:, g : g + 1],
+            )
+        w_codes = keep.tile([P, 2, NQ], U32, name="w_codes", align_bytes=64)
+        w_scales = keep.tile([P, 2, NQ], U8, name="w_scales", align_bytes=64)
+        for g in range(2):
+            turned = psum_tr.tile([P, PACK, P], F32, name="turn")
+            for t in range(PACK):
+                nc.tensor.transpose(turned[:, t, :], probs[:, g, t, :], ident_f[:])
+            w = keep.tile([P, NQ, PACK], BF16, name=f"w{g}", align_bytes=64)
+            nc.vector.tensor_tensor(
+                w[:],
+                turned[:].rearrange("s t q -> s q t"),
+                ts_cols[:, g, :].unsqueeze(1).to_broadcast([P, NQ, PACK]),
+                ALU.mult,
+            )
+            nc.vector.quantize_mx(
+                out=w_codes[:, g, :].bitcast(FP8X4), scales=w_scales[:, g, :], in_=w[:].rearrange("s q t -> s (q t)")
+            )
+        total = keep.tile([P, 1], F32, name="total")
+        nc.vector.tensor_tensor(total[:], sums[:, 0:1], sums[:, 1:2], ALU.add)
+        inverse = keep.tile([P, 1], F32, name="inverse")
+        nc.vector.reciprocal(inverse[:], total[:])
+
+        y = psum_s.tile([NQ, D], F32, name="y")
+        for g in range(2):
+            nc.tensor.matmul_mx(
+                out=y[:],
+                lhsT=w_codes[:, g, :].bitcast(FP8X4),
+                lhsT_scale=w_scales[:, g, :],
+                rhs=val_codes[:, g].rearrange("s t e -> s (t e)").bitcast(FP8X4),
+                rhs_scale=val_scales[:, g].rearrange("s t e -> s (t e)"),
+                start=(g == 0),
+                stop=(g == 1),
+            )
+        result = keep.tile([NQ, P, PACK], F32, name="result")
+        nc.vector.scalar_tensor_tensor(
+            result[:],
+            y[:].rearrange("q (t e) -> q e t", t=PACK),
+            inverse[:],
+            ch_sb[:].rearrange("q (e t) -> q e t", t=PACK),
+            ALU.mult,
+            ALU.mult,
+        )
+        nc.sync.dma_start(out=out[0], in_=result[:].rearrange("q e t -> q (e t)"))

@@ -26,9 +26,8 @@ def tile_attend_x_mla_alibi_srt_kernel(tc, qT, cT, ts, pos, slope, ch, offs, out
     nc = tc.nc
     with ExitStack() as ctx:
         keep = ctx.enter_context(tc.tile_pool(name="keep", bufs=1))
-        psum_tr = ctx.enter_context(tc.psum_pool(name="psum_tr", bufs=2))
-        psum_v = ctx.enter_context(tc.psum_pool(name="psum_v", bufs=2))
-        psum_s = ctx.enter_context(tc.psum_pool(name="psum_s", bufs=1))
+        psum2 = ctx.enter_context(tc.psum_pool(name="psum2", bufs=2))
+        psum1 = ctx.enter_context(tc.psum_pool(name="psum1", bufs=1))
 
         offsets = keep.tile([P, N // 16], U16, name="offsets")
         nc.sync.dma_start(offsets[:], offs)
@@ -39,7 +38,7 @@ def tile_attend_x_mla_alibi_srt_kernel(tc, qT, cT, ts, pos, slope, ch, offs, out
             planes.append(plane)
         tsw = keep.tile([P, T], F32, name="tsw")
         posw = keep.tile([P, T], F32, name="posw")
-        slope_sb = keep.tile([P, 1], F32, name="slope_sb")
+        slope_row = keep.tile([P, NQ], F32, name="slope_row")
         q_raw = keep.tile([P, PACK, NQ], F32, name="q_raw")
         ch_sb = keep.tile([P, D], F32, name="ch_sb")
 
@@ -49,7 +48,7 @@ def tile_attend_x_mla_alibi_srt_kernel(tc, qT, cT, ts, pos, slope, ch, offs, out
         make_identity(nc, ident_f[:])
         ident_b = keep.tile([P, P], BF16, name="ident_b")
         make_identity(nc, ident_b[:])
-        nc.scalar.dma_start(out=slope_sb[:], in_=slope[0])
+        nc.scalar.dma_start(out=slope_row[:], in_=slope.rearrange("b q o -> (b q o)").partition_broadcast(P))
         for window, held in ((tsw, (planes[1],)), (posw, (planes[2], planes[3], ch_sb))):
             nc.vector.memset(window[:, 0 : T // 2], 0.0)
             nc.gpsimd.memset(window[:, T // 2 : T], 0.0)
@@ -75,71 +74,63 @@ def tile_attend_x_mla_alibi_srt_kernel(tc, qT, cT, ts, pos, slope, ch, offs, out
             nc.vector.tensor_copy(picked[:], window[:].indirect(offsets[:]))
             return picked
 
-        def spread(picked, label):
+        def columns(picked, label):
             cols = keep.tile([P, 2, PACK], F32, name=f"{label}_cols")
-            for g in range(2):
-                turned = psum_tr.tile([P, PACK, P], F32, name="turn")
-                for t in range(PACK):
-                    nc.tensor.transpose(turned[:, t, :], picked[:, HALF * g + t : HALF * (g + 1) : PACK], ident_f[:])
-                nc.scalar.copy(cols[:, g, :], turned[:, :, 0])
-            rows = []
-            for g in range(2):
-                wide = psum_tr.tile([P, PACK, P], F32, name="turn")
-                for t in range(PACK):
-                    nc.tensor.transpose(wide[:, t, :], cols[:, g, t : t + 1].to_broadcast([P, P]), ident_f[:])
-                rows.append(wide)
-            return cols, rows
+            for h in range(2):
+                turned = psum1.tile([P, PACK, P], F32, name=f"raw{h}")
+                for j in range(PACK):
+                    nc.tensor.transpose(turned[:, j, :], picked[:, HALF * h + j : HALF * (h + 1) : PACK], ident_f[:])
+                nc.scalar.copy(cols[:, h, :], turned[:, :, 0])
+            return cols
 
-        latents = keep.tile([P, N, PACK], BF16, name="latents", align_bytes=64)
+        latents = keep.tile([P, 2, PACK, P, PACK], BF16, name="latents", align_bytes=64)
         val_codes = keep.tile([P, 2, PACK, P], U32, name="val_codes", align_bytes=64)
         val_scales = keep.tile([P, 2, PACK, P], U8, name="val_scales", align_bytes=64)
-
-        def gather(t, g):
-            cols = slice(HALF * g, HALF * (g + 1))
-            nc.vector.tensor_copy(latents[:, cols, t], planes[t][:].indirect(offsets[:, 32 * g : 32 * (g + 1)]))
-
-        def gather_whole(t):
-            nc.vector.tensor_copy(latents[:, :, t], planes[t][:].indirect(offsets[:]))
-
-        val_grouped = {}
+        values = []
+        for pair in range(2):
+            grouped = keep.tile([P, 2, 2, P, PACK], BF16, name=f"values{pair}", align_bytes=64)
+            values.append(grouped)
 
         def turn_values(t):
-            for g in range(2):
-                turned = psum_v.tile([P, PACK, P], BF16, name="turn_v")
+            turned = psum2.tile([P, 2, PACK, P], BF16, name="turn_v")
+            for h in range(2):
                 for j in range(PACK):
-                    nc.tensor.transpose(turned[:, j, :], latents[:, HALF * g + j : HALF * (g + 1) : PACK, t], ident_b[:])
-                grouped = keep.tile([P, P, PACK], BF16, name=f"val{t}_{g}", align_bytes=64)
-                nc.scalar.copy(grouped[:], turned[:].rearrange("s j e -> s e j"))
-                val_grouped[t, g] = grouped
+                    nc.tensor.transpose(
+                        turned[:, h, j, :], latents[:, h, j, :, t], ident_b[:]
+                    )
+            nc.scalar.copy(values[t // 2][:, :, t % 2], turned[:].rearrange("s h j e -> s h e j"))
 
-        def quantize_values(t):
-            for g in range(2):
+        def quantize_values(grouped, first):
+            for h in range(2):
                 nc.vector.quantize_mx(
-                    out=val_codes[:, g, t, :].bitcast(FP8X4),
-                    scales=val_scales[:, g, t, :],
-                    in_=val_grouped[t, g][:].rearrange("s e j -> s (e j)"),
+                    out=val_codes[:, h, first : first + 2, :].rearrange("s t e -> s (t e)").bitcast(FP8X4),
+                    scales=val_scales[:, h, first : first + 2, :].rearrange("s t e -> s (t e)"),
+                    in_=grouped[:, h].rearrange("s t e j -> s (t e j)"),
                 )
 
+        def gather_plane(t):
+            nc.vector.tensor_copy(
+                latents[:, :, :, :, t].rearrange("p h j i -> p h i j"), planes[t][:].indirect(offsets[:])
+            )
+
         ts_picked = pick(tsw, "ts")
-        gather_whole(0)
+        gather_plane(0)
         turn_values(0)
-        ts_cols, rows = spread(ts_picked, "ts")
-        ts_rows = keep.tile([P, 2, P, PACK], F32, name="ts_rows")
-        for g in range(2):
-            nc.scalar.copy(ts_rows[:, g], rows[g][:].rearrange("q t i -> q i t"))
-
-        gather_whole(1)
-        turn_values(1)
+        ts_cols = columns(ts_picked, "ts")
         pos_picked = pick(posw, "pos")
-        pos_cols, rows = spread(pos_picked, "pos")
-        bias = keep.tile([P, 2, P, PACK], F32, name="bias")
-        for g in range(2):
-            nc.scalar.activation(bias[:, g], rows[g][:].rearrange("q t i -> q i t"), ACT.Copy, scale=slope_sb[:])
+        gather_plane(1)
+        turn_values(1)
+        pos_cols = columns(pos_picked, "pos")
+        bias = keep.tile([P, 2, PACK, NQ], F32, name="bias")
+        for h in range(2):
+            nc.gpsimd.tensor_tensor(
+                bias[:, h],
+                slope_row[:].unsqueeze(1).to_broadcast([P, PACK, NQ]),
+                pos_cols[:, h, :].unsqueeze(2).to_broadcast([P, PACK, NQ]),
+                ALU.mult,
+            )
 
-        quantize_values(0)
-        gather_whole(2)
-        quantize_values(1)
-
+        gather_plane(2)
         key_codes = keep.tile([P, 2, HALF], U32, name="key_codes", align_bytes=64)
         key_scales = keep.tile([P, 2, HALF], U8, name="key_scales", align_bytes=64)
         q_grouped = keep.tile([P, NQ, PACK], BF16, name="q_grouped", align_bytes=64)
@@ -147,95 +138,106 @@ def tile_attend_x_mla_alibi_srt_kernel(tc, qT, cT, ts, pos, slope, ch, offs, out
         q_scales = keep.tile([P, NQ], U8, name="q_scales", align_bytes=64)
         nc.scalar.copy(q_grouped[:], q_raw[:].rearrange("p t q -> p q t"))
 
-        scores = []
-        for g in range(2):
-            gather(3, g)
-            if g == 0:
-                nc.vector.quantize_mx(
-                    out=q_codes[:].bitcast(FP8X4), scales=q_scales[:], in_=q_grouped[:].rearrange("p q t -> p (q t)")
-                )
-            nc.vector.quantize_mx(
-                out=key_codes[:, g, :].bitcast(FP8X4),
-                scales=key_scales[:, g, :],
-                in_=latents[:, HALF * g : HALF * (g + 1), :].rearrange("p i t -> p (i t)"),
-            )
-            acc = psum_s.tile([NQ, HALF], F32, name=f"scores{g}")
-            nc.tensor.matmul_mx(
-                out=acc[:],
-                lhsT=q_codes[:].bitcast(FP8X4),
-                lhsT_scale=q_scales[:],
-                rhs=key_codes[:, g, :].bitcast(FP8X4),
-                rhs_scale=key_scales[:, g, :],
-                start=True,
-                stop=True,
-            )
-            scores.append(acc)
+        gather_plane(3)
+        nc.vector.quantize_mx(
+            out=q_codes[:].bitcast(FP8X4), scales=q_scales[:], in_=q_grouped[:].rearrange("p q t -> p (q t)")
+        )
 
+        biased = keep.tile([P, 2, PACK, NQ], F32, name="biased")
+        raws = []
+        banks = []
+        for h in range(2):
+            nc.vector.quantize_mx(
+                out=key_codes[:, h, :].bitcast(FP8X4),
+                scales=key_scales[:, h, :],
+                in_=latents[:, h].rearrange("p j i t -> p (j i t)"),
+            )
+            raw = psum1.tile([P, PACK, NQ], F32, name=f"raw{h}")
+            for j in range(PACK):
+                block = slice(P * j, P * (j + 1))
+                nc.tensor.matmul_mx(
+                    out=raw[:, j, :],
+                    lhsT=key_codes[:, h, block].bitcast(FP8X4),
+                    lhsT_scale=key_scales[:, h, block],
+                    rhs=q_codes[:].bitcast(FP8X4),
+                    rhs_scale=q_scales[:],
+                    start=True,
+                    stop=True,
+                )
+            raws.append(raw)
+
+        for h in range(2):
+            bank = psum1.tile([NQ, PACK, P], F32, name=f"scores{h}")
+            for j in range(PACK):
+                nc.vector.scalar_tensor_tensor(
+                    biased[:, h, j, :], raws[h][:, j, :], ts_cols[:, h, j : j + 1], bias[:, h, j, :], ALU.mult, ALU.add
+                )
+                nc.tensor.transpose(bank[:, j, :], biased[:, h, j, :], ident_f[:])
+            banks.append(bank)
+
+        negated = keep.tile([NQ, PACK, P], F32, name="negated")
+        floors = keep.tile([NQ, 2], F32, name="floors")
+        nc.vector.tensor_scalar(
+            negated[:], banks[0][:], -1.0, None, ALU.mult, ALU.min, accum_out=floors[:, 0:1]
+        )
+        nc.vector.tensor_scalar(
+            negated[:], banks[1][:], -1.0, floors[:, 0:1], ALU.mult, ALU.min, accum_out=floors[:, 1:2]
+        )
+
+        quantize_values(values[0], 0)
         turn_values(2)
         turn_values(3)
+        quantize_values(values[1], 2)
 
-        scaled = keep.tile([P, 2, HALF], F32, name="scaled")
-        biased = keep.tile([P, 2, HALF], F32, name="biased")
-        peaks = keep.tile([P, 2], F32, name="peaks")
-        for g in range(2):
-            nc.vector.tensor_tensor(scaled[:, g, :], scores[g][:], ts_rows[:, g].rearrange("q i t -> q (i t)"), ALU.mult)
-            nc.vector.tensor_tensor(biased[:, g, :], scaled[:, g, :], bias[:, g].rearrange("q i t -> q (i t)"), ALU.add)
-            nc.vector.reduce_max(peaks[:, g : g + 1], biased[:, g, :], axis=AX.X)
-        minus_peak = keep.tile([P, 1], F32, name="minus_peak")
-        nc.vector.tensor_scalar(minus_peak[:], peaks[:, 0:1], peaks[:, 1:2], -1.0, ALU.max, ALU.mult)
-
-        quantize_values(2)
-        quantize_values(3)
-
-        probs = keep.tile([P, 2, PACK, P], F32, name="probs")
-        sums = keep.tile([P, 2], F32, name="sums")
-        for g in range(2):
+        probs = keep.tile([NQ, 2, PACK, P], F32, name="probs")
+        sums = keep.tile([NQ, 3], F32, name="sums")
+        for n, (h, j0, j1) in enumerate(((0, 0, 4), (1, 0, 2), (1, 2, 4))):
             nc.scalar.activation(
-                probs[:, g].rearrange("q t i -> q i t"),
-                biased[:, g, :].rearrange("q (i t) -> q i t", t=PACK),
-                ACT.Exp,
-                bias=minus_peak[:],
-                accum_out=sums[:, g : g + 1],
+                probs[:, h, j0:j1], banks[h][:, j0:j1, :], ACT.Exp, bias=floors[:, 1:2], accum_out=sums[:, n : n + 1]
             )
         w_codes = keep.tile([P, 2, NQ], U32, name="w_codes", align_bytes=64)
         w_scales = keep.tile([P, 2, NQ], U8, name="w_scales", align_bytes=64)
-        for g in range(2):
-            turned = psum_tr.tile([P, PACK, P], F32, name="turn")
+        weights = []
+        for h in range(2):
+            turned = psum2.tile([P, PACK, P], F32, name="turn")
             for t in range(PACK):
-                nc.tensor.transpose(turned[:, t, :], probs[:, g, t, :], ident_f[:])
-            w = keep.tile([P, NQ, PACK], BF16, name=f"w{g}", align_bytes=64)
+                nc.tensor.transpose(turned[:, t, :], probs[:, h, t, :], ident_f[:])
+            w = keep.tile([P, NQ, PACK], BF16, name=f"w{h}", align_bytes=64)
             nc.vector.tensor_tensor(
                 w[:],
                 turned[:].rearrange("s t q -> s q t"),
-                ts_cols[:, g, :].unsqueeze(1).to_broadcast([P, NQ, PACK]),
+                ts_cols[:, h, :].unsqueeze(1).to_broadcast([P, NQ, PACK]),
                 ALU.mult,
             )
+            weights.append(w)
+        for h in range(2):
             nc.vector.quantize_mx(
-                out=w_codes[:, g, :].bitcast(FP8X4), scales=w_scales[:, g, :], in_=w[:].rearrange("s q t -> s (q t)")
+                out=w_codes[:, h, :].bitcast(FP8X4), scales=w_scales[:, h, :], in_=weights[h][:].rearrange("s q t -> s (q t)")
             )
         total = keep.tile([P, 1], F32, name="total")
-        nc.vector.tensor_tensor(total[:], sums[:, 0:1], sums[:, 1:2], ALU.add)
+        nc.vector.reduce_sum(total[:], sums[:], axis=AX.X)
         inverse = keep.tile([P, 1], F32, name="inverse")
         nc.vector.reciprocal(inverse[:], total[:])
 
-        y = psum_s.tile([NQ, D], F32, name="y")
-        for g in range(2):
+        y = psum1.tile([NQ, D], F32, name="raw0")
+        for h in range(2):
             nc.tensor.matmul_mx(
                 out=y[:],
-                lhsT=w_codes[:, g, :].bitcast(FP8X4),
-                lhsT_scale=w_scales[:, g, :],
-                rhs=val_codes[:, g].rearrange("s t e -> s (t e)").bitcast(FP8X4),
-                rhs_scale=val_scales[:, g].rearrange("s t e -> s (t e)"),
-                start=(g == 0),
-                stop=(g == 1),
+                lhsT=w_codes[:, h, :].bitcast(FP8X4),
+                lhsT_scale=w_scales[:, h, :],
+                rhs=val_codes[:, h].rearrange("s t e -> s (t e)").bitcast(FP8X4),
+                rhs_scale=val_scales[:, h].rearrange("s t e -> s (t e)"),
+                start=(h == 0),
+                stop=(h == 1),
             )
         result = keep.tile([NQ, P, PACK], F32, name="result")
-        nc.vector.scalar_tensor_tensor(
-            result[:],
-            y[:].rearrange("q (t e) -> q e t", t=PACK),
-            inverse[:],
-            ch_sb[:].rearrange("q (e t) -> q e t", t=PACK),
-            ALU.mult,
-            ALU.mult,
-        )
-        nc.sync.dma_start(out=out[0], in_=result[:].rearrange("q e t -> q (e t)"))
+        y_view = y[:].rearrange("q (t e) -> q e t", t=PACK)
+        ch_view = ch_sb[:].rearrange("q (e t) -> q e t", t=PACK)
+        for n, queue in enumerate((nc.scalar, nc.sync)):
+            part = slice(P // 2 * n, P // 2 * (n + 1))
+            nc.vector.scalar_tensor_tensor(
+                result[:, part], y_view[:, part], inverse[:], ch_view[:, part], ALU.mult, ALU.mult
+            )
+            queue.dma_start(
+                out=out[0][:, D // 2 * n : D // 2 * (n + 1)], in_=result[:, part].rearrange("q e t -> q (e t)")
+            )

@@ -46,24 +46,20 @@ def tile_attend_x_mla_alibi_srt_kernel(tc, qT, cT, ts, pos, slope, ch, offs, out
         nc.sync.dma_start(out=planes[0][:], in_=c_view[0])
         ident_f = keep.tile([P, P], F32, name="ident_f")
         make_identity(nc, ident_f[:])
-        ident_b = keep.tile([P, P], BF16, name="ident_b")
-        make_identity(nc, ident_b[:])
         nc.scalar.dma_start(out=slope_row[:], in_=slope.rearrange("b q o -> (b q o)").partition_broadcast(P))
-        for window, held in ((tsw, (planes[1],)), (posw, (planes[2], planes[3], ch_sb))):
-            nc.vector.memset(window[:, 0 : T // 2], 0.0)
-            nc.gpsimd.memset(window[:, T // 2 : T], 0.0)
-            for late in held:
-                nc.vector.memset(late[:, 0:8], 0.0)
-                nc.gpsimd.memset(late[:, 8:16], 0.0)
-        nc.vector.memset(q_raw[:, 0, 0:8], 0.0)
+        nc.vector.memset(tsw[:], 0.0)
+        nc.vector.memset(planes[1][:, 0:8], 0.0)
         nc.sync.dma_start(out=tsw[0:1, :], in_=ts[0:1, :])
         nc.sync.dma_start(out=planes[1][:], in_=c_view[1])
+        nc.vector.memset(posw[:], 0.0)
+        for late in (planes[2], planes[3], ch_sb):
+            nc.vector.memset(late[:, 0:8], 0.0)
+        nc.vector.memset(q_raw[:, 0, 0:8], 0.0)
         nc.sync.dma_start(out=posw[0:1, :], in_=pos[0:1, :])
         nc.sync.dma_start(out=planes[2][:], in_=c_view[2])
         nc.sync.dma_start(out=planes[3][:], in_=c_view[3])
         nc.sync.dma_start(out=q_raw[:], in_=qT[0].rearrange("(p t) q -> p t q", t=PACK))
         nc.sync.dma_start(out=ch_sb[:], in_=ch)
-
 
         warm = keep.tile([P, 1], F32, name="warm")
         nc.gpsimd.memset(warm[:], 0.0)
@@ -74,16 +70,21 @@ def tile_attend_x_mla_alibi_srt_kernel(tc, qT, cT, ts, pos, slope, ch, offs, out
             nc.vector.tensor_copy(picked[:], window[:].indirect(offsets[:]))
             return picked
 
-        def columns(picked, label):
+        def columns(picked, label, strided):
             cols = keep.tile([P, 2, PACK], F32, name=f"{label}_cols")
             for h in range(2):
-                turned = psum1.tile([P, PACK, P], F32, name=f"raw{h}")
+                turned = psum1.tile([P, PACK, P], F32, name=f"raw{h}" if strided else f"scores{h}")
                 for j in range(PACK):
-                    nc.tensor.transpose(turned[:, j, :], picked[:, HALF * h + j : HALF * (h + 1) : PACK], ident_f[:])
+                    if strided:
+                        block = picked[:, HALF * h + j : HALF * (h + 1) : PACK]
+                    else:
+                        block = picked[:, HALF * h + P * j : HALF * h + P * (j + 1)]
+                    nc.tensor.transpose(turned[:, j, :], block, ident_f[:])
                 nc.scalar.copy(cols[:, h, :], turned[:, :, 0])
             return cols
 
-        latents = keep.tile([P, 2, PACK, P, PACK], BF16, name="latents", align_bytes=64)
+        gathered = keep.tile([P, PACK, N], F32, name="gathered")
+        latents = keep.tile([P, N, PACK], BF16, name="latents", align_bytes=64)
         val_codes = keep.tile([P, 2, PACK, P], U32, name="val_codes", align_bytes=64)
         val_scales = keep.tile([P, 2, PACK, P], U8, name="val_scales", align_bytes=64)
         values = []
@@ -92,53 +93,56 @@ def tile_attend_x_mla_alibi_srt_kernel(tc, qT, cT, ts, pos, slope, ch, offs, out
             values.append(grouped)
 
         def turn_values(t):
-            turned = psum2.tile([P, 2, PACK, P], BF16, name="turn_v")
             for h in range(2):
+                turned = psum2.tile([P, PACK, P], F32, name="turn")
                 for j in range(PACK):
-                    nc.tensor.transpose(
-                        turned[:, h, j, :], latents[:, h, j, :, t], ident_b[:]
-                    )
-            nc.scalar.copy(values[t // 2][:, :, t % 2], turned[:].rearrange("s h j e -> s h e j"))
+                    nc.tensor.transpose(turned[:, j, :], gathered[:, t, HALF * h + j : HALF * (h + 1) : PACK], ident_f[:])
+                nc.scalar.copy(values[t // 2][:, h, t % 2], turned[:].rearrange("s j e -> s e j"))
 
-        def quantize_values(grouped, first):
+        def quantize_values(pair):
             for h in range(2):
                 nc.vector.quantize_mx(
-                    out=val_codes[:, h, first : first + 2, :].rearrange("s t e -> s (t e)").bitcast(FP8X4),
-                    scales=val_scales[:, h, first : first + 2, :].rearrange("s t e -> s (t e)"),
-                    in_=grouped[:, h].rearrange("s t e j -> s (t e j)"),
+                    out=val_codes[:, h, 2 * pair : 2 * pair + 2, :].rearrange("s t e -> s (t e)").bitcast(FP8X4),
+                    scales=val_scales[:, h, 2 * pair : 2 * pair + 2, :].rearrange("s t e -> s (t e)"),
+                    in_=values[pair][:, h].rearrange("s t e j -> s (t e j)"),
                 )
 
-        def gather_plane(t):
-            nc.vector.tensor_copy(
-                latents[:, :, :, :, t].rearrange("p h j i -> p h i j"), planes[t][:].indirect(offsets[:])
-            )
+        def interleave(copy, first, h):
+            cols = slice(HALF * h, HALF * (h + 1))
+            copy(latents[:, cols, first : first + 2], gathered[:, first : first + 2, cols].rearrange("p t i -> p i t"))
 
         ts_picked = pick(tsw, "ts")
-        gather_plane(0)
+        nc.vector.tensor_copy(gathered[:, 0, :], planes[0][:].indirect(offsets[:]))
+        ts_cols = columns(ts_picked, "ts", False)
+        ts_spread = columns(ts_picked, "ts_spread", True)
         turn_values(0)
-        ts_cols = columns(ts_picked, "ts")
         pos_picked = pick(posw, "pos")
-        gather_plane(1)
+        nc.vector.tensor_copy(gathered[:, 1, :], planes[1][:].indirect(offsets[:]))
+        pos_cols = columns(pos_picked, "pos", False)
         turn_values(1)
-        pos_cols = columns(pos_picked, "pos")
         bias = keep.tile([P, 2, PACK, NQ], F32, name="bias")
         for h in range(2):
-            nc.gpsimd.tensor_tensor(
-                bias[:, h],
-                slope_row[:].unsqueeze(1).to_broadcast([P, PACK, NQ]),
-                pos_cols[:, h, :].unsqueeze(2).to_broadcast([P, PACK, NQ]),
-                ALU.mult,
-            )
+            for j in range(PACK):
+                nc.scalar.activation(bias[:, h, j, :], slope_row[:], ACT.Copy, scale=pos_cols[:, h, j : j + 1])
+        interleave(nc.vector.tensor_copy, 0, 0)
+        interleave(nc.vector.tensor_copy, 0, 1)
+        nc.vector.tensor_copy(gathered[:, 2, :], planes[2][:].indirect(offsets[:]))
+        turn_values(2)
+        quantize_values(0)
 
-        gather_plane(2)
         key_codes = keep.tile([P, 2, HALF], U32, name="key_codes", align_bytes=64)
         key_scales = keep.tile([P, 2, HALF], U8, name="key_scales", align_bytes=64)
         q_grouped = keep.tile([P, NQ, PACK], BF16, name="q_grouped", align_bytes=64)
         q_codes = keep.tile([P, NQ], U32, name="q_codes", align_bytes=64)
         q_scales = keep.tile([P, NQ], U8, name="q_scales", align_bytes=64)
-        nc.scalar.copy(q_grouped[:], q_raw[:].rearrange("p t q -> p q t"))
 
-        gather_plane(3)
+        for h in range(2):
+            nc.vector.tensor_copy(
+                gathered[:, 3, HALF * h : HALF * (h + 1)], planes[3][:].indirect(offsets[:, 32 * h : 32 * (h + 1)])
+            )
+        nc.scalar.copy(q_grouped[:], q_raw[:].rearrange("p t q -> p q t"))
+        interleave(nc.scalar.copy, 2, 0)
+        interleave(nc.vector.tensor_copy, 2, 1)
         nc.vector.quantize_mx(
             out=q_codes[:].bitcast(FP8X4), scales=q_scales[:], in_=q_grouped[:].rearrange("p q t -> p (q t)")
         )
@@ -150,7 +154,7 @@ def tile_attend_x_mla_alibi_srt_kernel(tc, qT, cT, ts, pos, slope, ch, offs, out
             nc.vector.quantize_mx(
                 out=key_codes[:, h, :].bitcast(FP8X4),
                 scales=key_scales[:, h, :],
-                in_=latents[:, h].rearrange("p j i t -> p (j i t)"),
+                in_=latents[:, HALF * h : HALF * (h + 1), :].rearrange("p i t -> p (i t)"),
             )
             raw = psum1.tile([P, PACK, NQ], F32, name=f"raw{h}")
             for j in range(PACK):
@@ -184,16 +188,18 @@ def tile_attend_x_mla_alibi_srt_kernel(tc, qT, cT, ts, pos, slope, ch, offs, out
             negated[:], banks[1][:], -1.0, floors[:, 0:1], ALU.mult, ALU.min, accum_out=floors[:, 1:2]
         )
 
-        quantize_values(values[0], 0)
-        turn_values(2)
         turn_values(3)
-        quantize_values(values[1], 2)
+        quantize_values(1)
 
         probs = keep.tile([NQ, 2, PACK, P], F32, name="probs")
-        sums = keep.tile([NQ, 3], F32, name="sums")
-        for n, (h, j0, j1) in enumerate(((0, 0, 4), (1, 0, 2), (1, 2, 4))):
+        sums = keep.tile([NQ, 2], F32, name="sums")
+        for h in range(2):
             nc.scalar.activation(
-                probs[:, h, j0:j1], banks[h][:, j0:j1, :], ACT.Exp, bias=floors[:, 1:2], accum_out=sums[:, n : n + 1]
+                probs[:, h].rearrange("q t i -> q i t"),
+                banks[h][:].rearrange("q j m -> q (j m)").rearrange("q (i t) -> q i t", t=PACK),
+                ACT.Exp,
+                bias=floors[:, 1:2],
+                accum_out=sums[:, h : h + 1],
             )
         w_codes = keep.tile([P, 2, NQ], U32, name="w_codes", align_bytes=64)
         w_scales = keep.tile([P, 2, NQ], U8, name="w_scales", align_bytes=64)
@@ -206,7 +212,7 @@ def tile_attend_x_mla_alibi_srt_kernel(tc, qT, cT, ts, pos, slope, ch, offs, out
             nc.vector.tensor_tensor(
                 w[:],
                 turned[:].rearrange("s t q -> s q t"),
-                ts_cols[:, h, :].unsqueeze(1).to_broadcast([P, NQ, PACK]),
+                ts_spread[:, h, :].unsqueeze(1).to_broadcast([P, NQ, PACK]),
                 ALU.mult,
             )
             weights.append(w)

@@ -38,6 +38,7 @@ def tile_attend_x_mla_alibi_srt_kernel(tc, qT, cT, ts, pos, slope, ch, offs, out
             planes.append(plane)
         tsw = keep.tile([P, T], F32, name="tsw")
         posw = keep.tile([P, T], F32, name="posw")
+        slope_col = keep.tile([NQ, 1], F32, name="slope_col")
         slope_row = keep.tile([P, NQ], F32, name="slope_row")
         q_raw = keep.tile([P, PACK, NQ], F32, name="q_raw")
         ch_sb = keep.tile([P, D], F32, name="ch_sb")
@@ -46,7 +47,7 @@ def tile_attend_x_mla_alibi_srt_kernel(tc, qT, cT, ts, pos, slope, ch, offs, out
         nc.sync.dma_start(out=planes[0][:], in_=c_view[0])
         ident_f = keep.tile([P, P], F32, name="ident_f")
         make_identity(nc, ident_f[:])
-        nc.scalar.dma_start(out=slope_row[:], in_=slope.rearrange("b q o -> (b q o)").partition_broadcast(P))
+        nc.scalar.dma_start(out=slope_col[:], in_=slope[0])
         nc.vector.memset(tsw[:], 0.0)
         nc.vector.memset(planes[1][:, 0:8], 0.0)
         nc.sync.dma_start(out=tsw[0:1, :], in_=ts[0:1, :])
@@ -110,6 +111,10 @@ def tile_attend_x_mla_alibi_srt_kernel(tc, qT, cT, ts, pos, slope, ch, offs, out
         def interleave(copy, first, h):
             cols = slice(HALF * h, HALF * (h + 1))
             copy(latents[:, cols, first : first + 2], gathered[:, first : first + 2, cols].rearrange("p t i -> p i t"))
+
+        slope_turned = psum1.tile([P, PACK, NQ], F32, name="scores0")
+        nc.tensor.transpose(slope_turned[:, 0, :], slope_col[:].to_broadcast([NQ, P]), ident_f[:])
+        nc.scalar.copy(slope_row[:], slope_turned[:, 0, :])
 
         ts_picked = pick(tsw, "ts")
         nc.vector.tensor_copy(gathered[:, 0, :], planes[0][:].indirect(offsets[:]))

@@ -56,7 +56,7 @@ def tile_attend_x_mla_alibi_srt_kernel(tc, qT, cT, ts, pos, slope, ch, offs, out
         for late in (planes[2], planes[3], ch_sb):
             nc.vector.memset(late[:, 0:8], 0.0)
         nc.vector.memset(q_raw[:, 0, 0:8], 0.0)
-        nc.sync.dma_start(out=posw[0:1, :], in_=pos[0:1, :])
+        nc.sync.dma_start(out=posw[64:65, :], in_=pos[0:1, :])
         nc.sync.dma_start(out=planes[2][:], in_=c_view[2])
         nc.sync.dma_start(out=planes[3][:], in_=c_view[3])
         nc.sync.dma_start(out=q_raw[:], in_=qT[0].rearrange("(p t) q -> p t q", t=PACK))
@@ -71,7 +71,7 @@ def tile_attend_x_mla_alibi_srt_kernel(tc, qT, cT, ts, pos, slope, ch, offs, out
             nc.vector.tensor_copy(picked[:], window[:].indirect(offsets[:]))
             return picked
 
-        def columns(picked, label, strided):
+        def columns(picked, row, label, strided):
             cols = keep.tile([P, 2, PACK], F32, name=f"{label}_cols")
             for h in range(2):
                 turned = psum1.tile([P, PACK, P], F32, name=f"raw{h}" if strided else f"scores{h}")
@@ -81,16 +81,16 @@ def tile_attend_x_mla_alibi_srt_kernel(tc, qT, cT, ts, pos, slope, ch, offs, out
                     else:
                         block = picked[:, HALF * h + P * j : HALF * h + P * (j + 1)]
                     nc.tensor.transpose(turned[:, j, :], block, ident_f[:])
-                nc.scalar.copy(cols[:, h, :], turned[:, :, 0])
+                nc.scalar.copy(cols[:, h, :], turned[:, :, row])
             return cols
 
         gathered = keep.tile([P, PACK, N], F32, name="gathered")
         latents = keep.tile([P, N, PACK], BF16, name="latents", align_bytes=64)
-        val_codes = keep.tile([P, 2, PACK, P], U32, name="val_codes", align_bytes=64)
-        val_scales = keep.tile([P, 2, PACK, P], U8, name="val_scales", align_bytes=64)
+        val_codes = keep.tile([P, 2, 2, PACK, P // 2], U32, name="val_codes", align_bytes=64)
+        val_scales = keep.tile([P, 2, 2, PACK, P // 2], U8, name="val_scales", align_bytes=64)
         values = []
         for pair in range(2):
-            grouped = keep.tile([P, 2, 2, P, PACK], BF16, name=f"values{pair}", align_bytes=64)
+            grouped = keep.tile([P, 2, 2, 2, P // 2, PACK], BF16, name=f"values{pair}", align_bytes=64)
             values.append(grouped)
 
         def turn_values(t):
@@ -98,15 +98,16 @@ def tile_attend_x_mla_alibi_srt_kernel(tc, qT, cT, ts, pos, slope, ch, offs, out
                 turned = psum2.tile([P, PACK, P], F32, name="turn")
                 for j in range(PACK):
                     nc.tensor.transpose(turned[:, j, :], gathered[:, t, HALF * h + j : HALF * (h + 1) : PACK], ident_f[:])
-                nc.scalar.copy(values[t // 2][:, h, t % 2], turned[:].rearrange("s j e -> s e j"))
+                nc.scalar.copy(values[t // 2][:, h, :, t % 2], turned[:].rearrange("s j (v e) -> s v e j", v=2))
 
         def quantize_values(pair):
             for h in range(2):
-                nc.vector.quantize_mx(
-                    out=val_codes[:, h, 2 * pair : 2 * pair + 2, :].rearrange("s t e -> s (t e)").bitcast(FP8X4),
-                    scales=val_scales[:, h, 2 * pair : 2 * pair + 2, :].rearrange("s t e -> s (t e)"),
-                    in_=values[pair][:, h].rearrange("s t e j -> s (t e j)"),
-                )
+                for v in range(2):
+                    nc.vector.quantize_mx(
+                        out=val_codes[:, h, v, 2 * pair : 2 * pair + 2, :].rearrange("s t e -> s (t e)").bitcast(FP8X4),
+                        scales=val_scales[:, h, v, 2 * pair : 2 * pair + 2, :].rearrange("s t e -> s (t e)"),
+                        in_=values[pair][:, h, v].rearrange("s t e j -> s (t e j)"),
+                    )
 
         def interleave(copy, first, h):
             cols = slice(HALF * h, HALF * (h + 1))
@@ -118,12 +119,12 @@ def tile_attend_x_mla_alibi_srt_kernel(tc, qT, cT, ts, pos, slope, ch, offs, out
 
         ts_picked = pick(tsw, "ts")
         nc.vector.tensor_copy(gathered[:, 0, :], planes[0][:].indirect(offsets[:]))
-        ts_cols = columns(ts_picked, "ts", False)
-        ts_spread = columns(ts_picked, "ts_spread", True)
+        ts_cols = columns(ts_picked, 0, "ts", False)
+        ts_spread = columns(ts_picked, 0, "ts_spread", True)
         turn_values(0)
         pos_picked = pick(posw, "pos")
         nc.vector.tensor_copy(gathered[:, 1, :], planes[1][:].indirect(offsets[:]))
-        pos_cols = columns(pos_picked, "pos", False)
+        pos_cols = columns(pos_picked, 64, "pos", False)
         turn_values(1)
         bias = keep.tile([P, 2, PACK, NQ], F32, name="bias")
         for h in range(2):
@@ -197,14 +198,14 @@ def tile_attend_x_mla_alibi_srt_kernel(tc, qT, cT, ts, pos, slope, ch, offs, out
         quantize_values(1)
 
         probs = keep.tile([NQ, 2, PACK, P], F32, name="probs")
-        sums = keep.tile([NQ, 2], F32, name="sums")
-        for h in range(2):
+        sums = keep.tile([NQ, 3], F32, name="sums")
+        for n, (h, j0, j1) in enumerate(((0, 0, 4), (1, 0, 2), (1, 2, 4))):
             nc.scalar.activation(
-                probs[:, h].rearrange("q t i -> q i t"),
-                banks[h][:].rearrange("q j m -> q (j m)").rearrange("q (i t) -> q i t", t=PACK),
+                probs[:, h, j0:j1],
+                banks[h][:].rearrange("q b m -> q (b m)").rearrange("q (i j) -> q j i", j=PACK)[:, j0:j1],
                 ACT.Exp,
                 bias=floors[:, 1:2],
-                accum_out=sums[:, h : h + 1],
+                accum_out=sums[:, n : n + 1],
             )
         w_codes = keep.tile([P, 2, NQ], U32, name="w_codes", align_bytes=64)
         w_scales = keep.tile([P, 2, NQ], U8, name="w_scales", align_bytes=64)
@@ -230,25 +231,33 @@ def tile_attend_x_mla_alibi_srt_kernel(tc, qT, cT, ts, pos, slope, ch, offs, out
         inverse = keep.tile([P, 1], F32, name="inverse")
         nc.vector.reciprocal(inverse[:], total[:])
 
-        y = psum1.tile([NQ, D], F32, name="raw0")
+        outputs = []
+        for v in range(2):
+            y = psum1.tile([NQ, D // 2], F32, name=f"raw{v}")
+            outputs.append(y)
         for h in range(2):
-            nc.tensor.matmul_mx(
-                out=y[:],
-                lhsT=w_codes[:, h, :].bitcast(FP8X4),
-                lhsT_scale=w_scales[:, h, :],
-                rhs=val_codes[:, h].rearrange("s t e -> s (t e)").bitcast(FP8X4),
-                rhs_scale=val_scales[:, h].rearrange("s t e -> s (t e)"),
-                start=(h == 0),
-                stop=(h == 1),
-            )
+            for v in range(2):
+                nc.tensor.matmul_mx(
+                    out=outputs[v][:],
+                    lhsT=w_codes[:, h, :].bitcast(FP8X4),
+                    lhsT_scale=w_scales[:, h, :],
+                    rhs=val_codes[:, h, v].rearrange("s t e -> s (t e)").bitcast(FP8X4),
+                    rhs_scale=val_scales[:, h, v].rearrange("s t e -> s (t e)"),
+                    start=(h == 0),
+                    stop=(h == 1),
+                )
         result = keep.tile([NQ, P, PACK], F32, name="result")
-        y_view = y[:].rearrange("q (t e) -> q e t", t=PACK)
         ch_view = ch_sb[:].rearrange("q (e t) -> q e t", t=PACK)
-        for n, queue in enumerate((nc.scalar, nc.sync)):
-            part = slice(P // 2 * n, P // 2 * (n + 1))
+        for v, queue in enumerate((nc.scalar, nc.sync)):
+            part = slice(P // 2 * v, P // 2 * (v + 1))
             nc.vector.scalar_tensor_tensor(
-                result[:, part], y_view[:, part], inverse[:], ch_view[:, part], ALU.mult, ALU.mult
+                result[:, part],
+                outputs[v][:].rearrange("q (t e) -> q e t", t=PACK),
+                inverse[:],
+                ch_view[:, part],
+                ALU.mult,
+                ALU.mult,
             )
             queue.dma_start(
-                out=out[0][:, D // 2 * n : D // 2 * (n + 1)], in_=result[:, part].rearrange("q e t -> q (e t)")
+                out=out[0][:, D // 2 * v : D // 2 * (v + 1)], in_=result[:, part].rearrange("q e t -> q (e t)")
             )

from contextlib import ExitStack

import concourse.mybir as mybir
from concourse.masks import make_identity

NQ, N, T, D = 128, 1024, 4096, 512
P = 128
PACK = 4
HALF = 512

F32 = mybir.dt.float32
BF16 = mybir.dt.bfloat16
U32 = mybir.dt.uint32
U16 = mybir.dt.uint16
U8 = mybir.dt.uint8
FP8X4 = mybir.dt.float8_e4m3fn_x4
ACT = mybir.ActivationFunctionType
ALU = mybir.AluOpType
AX = mybir.AxisListType

FLOPS = 2 * 2 * NQ * N * D
BYTES = 4 * (D * T + D * NQ + 2 * T + NQ + D + NQ * D) + 2 * P * N // 16


def tile_attend_x_mla_alibi_srt_kernel(tc, qT, cT, ts, pos, slope, ch, offs, out):
    nc = tc.nc
    with ExitStack() as ctx:
        keep = ctx.enter_context(tc.tile_pool(name="keep", bufs=1))
        psum2 = ctx.enter_context(tc.psum_pool(name="psum2", bufs=2))
        psum1 = ctx.enter_context(tc.psum_pool(name="psum1", bufs=1))

        offsets = keep.tile([P, N // 16], U16, name="offsets")
        nc.sync.dma_start(offsets[:], offs)

        planes = []
        for t in range(PACK):
            plane = keep.tile([P, T], F32, name=f"plane{t}")
            planes.append(plane)
        tsw = keep.tile([P, T], F32, name="tsw")
        posw = keep.tile([P, T], F32, name="posw")
        slope_col = keep.tile([NQ, 1], F32, name="slope_col")
        slope_row = keep.tile([P, NQ], F32, name="slope_row")
        q_raw = keep.tile([P, PACK, NQ], F32, name="q_raw")
        ch_sb = keep.tile([P, D], F32, name="ch_sb")

        c_view = cT.rearrange("(p t) n -> t p n", t=PACK)
        nc.sync.dma_start(out=planes[0][:], in_=c_view[0])
        ident_f = keep.tile([P, P], F32, name="ident_f")
        make_identity(nc, ident_f[:])
        nc.scalar.dma_start(out=slope_col[:], in_=slope[0])
        nc.vector.memset(tsw[:], 0.0)
        nc.vector.memset(planes[1][:, 0:8], 0.0)
        nc.sync.dma_start(out=tsw[0:1, :], in_=ts[0:1, :])
        nc.sync.dma_start(out=planes[1][:], in_=c_view[1])
        nc.vector.memset(posw[:], 0.0)
        for late in (planes[2], planes[3], ch_sb):
            nc.vector.memset(late[:, 0:8], 0.0)
        nc.vector.memset(q_raw[:, 0, 0:8], 0.0)
        nc.sync.dma_start(out=posw[64:65, :], in_=pos[0:1, :])
        nc.sync.dma_start(out=planes[2][:], in_=c_view[2])
        nc.sync.dma_start(out=planes[3][:], in_=c_view[3])
        nc.sync.dma_start(out=q_raw[:], in_=qT[0].rearrange("(p t) q -> p t q", t=PACK))
        nc.sync.dma_start(out=ch_sb[:], in_=ch)

        warm = keep.tile([P, 1], F32, name="warm")
        nc.gpsimd.memset(warm[:], 0.0)
        nc.scalar.activation(warm[:], warm[:], ACT.Exp)

        def pick(window, label):
            picked = keep.tile([P, N], F32, name=f"{label}_picked")
            nc.vector.tensor_copy(picked[:], window[:].indirect(offsets[:]))
            return picked

        def columns(picked, row, label, strided):
            cols = keep.tile([P, 2, PACK], F32, name=f"{label}_cols")
            for h in range(2):
                turned = psum1.tile([P, PACK, P], F32, name=f"raw{h}" if strided else f"scores{h}")
                for j in range(PACK):
                    if strided:
                        block = picked[:, HALF * h + j : HALF * (h + 1) : PACK]
                    else:
                        block = picked[:, HALF * h + P * j : HALF * h + P * (j + 1)]
                    nc.tensor.transpose(turned[:, j, :], block, ident_f[:])
                nc.scalar.copy(cols[:, h, :], turned[:, :, row])
            return cols

        gathered = keep.tile([P, PACK, N], F32, name="gathered")
        latents = keep.tile([P, N, PACK], BF16, name="latents", align_bytes=64)
        val_codes = keep.tile([P, 2, 2, PACK, P // 2], U32, name="val_codes", align_bytes=64)
        val_scales = keep.tile([P, 2, 2, PACK, P // 2], U8, name="val_scales", align_bytes=64)
        values = []
        for pair in range(2):
            grouped = keep.tile([P, 2, 2, 2, P // 2, PACK], BF16, name=f"values{pair}", align_bytes=64)
            values.append(grouped)

        def turn_values(t):
            for h in range(2):
                turned = psum2.tile([P, PACK, P], F32, name="turn")
                for j in range(PACK):
                    nc.tensor.transpose(turned[:, j, :], gathered[:, t, HALF * h + j : HALF * (h + 1) : PACK], ident_f[:])
                nc.scalar.copy(values[t // 2][:, h, :, t % 2], turned[:].rearrange("s j (v e) -> s v e j", v=2))

        def quantize_values(pair):
            for h in range(2):
                for v in range(2):
                    nc.vector.quantize_mx(
                        out=val_codes[:, h, v, 2 * pair : 2 * pair + 2, :].rearrange("s t e -> s (t e)").bitcast(FP8X4),
                        scales=val_scales[:, h, v, 2 * pair : 2 * pair + 2, :].rearrange("s t e -> s (t e)"),
                        in_=values[pair][:, h, v].rearrange("s t e j -> s (t e j)"),
                    )

        def interleave(copy, first, h):
            cols = slice(HALF * h, HALF * (h + 1))
            copy(latents[:, cols, first : first + 2], gathered[:, first : first + 2, cols].rearrange("p t i -> p i t"))

        slope_turned = psum1.tile([P, PACK, NQ], F32, name="scores0")
        nc.tensor.transpose(slope_turned[:, 0, :], slope_col[:].to_broadcast([NQ, P]), ident_f[:])
        nc.scalar.copy(slope_row[:], slope_turned[:, 0, :])

        ts_picked = pick(tsw, "ts")
        nc.vector.tensor_copy(gathered[:, 0, :], planes[0][:].indirect(offsets[:]))
        ts_cols = columns(ts_picked, 0, "ts", False)
        ts_spread = columns(ts_picked, 0, "ts_spread", True)
        turn_values(0)
        pos_picked = pick(posw, "pos")
        nc.vector.tensor_copy(gathered[:, 1, :], planes[1][:].indirect(offsets[:]))
        pos_cols = columns(pos_picked, 64, "pos", False)
        turn_values(1)
        bias = keep.tile([P, 2, PACK, NQ], F32, name="bias")
        for h in range(2):
            for j in range(PACK):
                nc.scalar.activation(bias[:, h, j, :], slope_row[:], ACT.Copy, scale=pos_cols[:, h, j : j + 1])
        interleave(nc.vector.tensor_copy, 0, 0)
        interleave(nc.vector.tensor_copy, 0, 1)
        nc.vector.tensor_copy(gathered[:, 2, :], planes[2][:].indirect(offsets[:]))
        turn_values(2)
        quantize_values(0)

        key_codes = keep.tile([P, 2, HALF], U32, name="key_codes", align_bytes=64)
        key_scales = keep.tile([P, 2, HALF], U8, name="key_scales", align_bytes=64)
        q_grouped = keep.tile([P, NQ, PACK], BF16, name="q_grouped", align_bytes=64)
        q_codes = keep.tile([P, NQ], U32, name="q_codes", align_bytes=64)
        q_scales = keep.tile([P, NQ], U8, name="q_scales", align_bytes=64)

        for h in range(2):
            nc.vector.tensor_copy(
                gathered[:, 3, HALF * h : HALF * (h + 1)], planes[3][:].indirect(offsets[:, 32 * h : 32 * (h + 1)])
            )
        nc.scalar.copy(q_grouped[:], q_raw[:].rearrange("p t q -> p q t"))
        interleave(nc.scalar.copy, 2, 0)
        interleave(nc.vector.tensor_copy, 2, 1)
        nc.vector.quantize_mx(
            out=q_codes[:].bitcast(FP8X4), scales=q_scales[:], in_=q_grouped[:].rearrange("p q t -> p (q t)")
        )

        biased = keep.tile([P, 2, PACK, NQ], F32, name="biased")
        raws = []
        banks = []
        for h in range(2):
            nc.vector.quantize_mx(
                out=key_codes[:, h, :].bitcast(FP8X4),
                scales=key_scales[:, h, :],
                in_=latents[:, HALF * h : HALF * (h + 1), :].rearrange("p i t -> p (i t)"),
            )
            raw = psum1.tile([P, PACK, NQ], F32, name=f"raw{h}")
            for j in range(PACK):
                block = slice(P * j, P * (j + 1))
                nc.tensor.matmul_mx(
                    out=raw[:, j, :],
                    lhsT=key_codes[:, h, block].bitcast(FP8X4),
                    lhsT_scale=key_scales[:, h, block],
                    rhs=q_codes[:].bitcast(FP8X4),
                    rhs_scale=q_scales[:],
                    start=True,
                    stop=True,
                )
            raws.append(raw)

        for h in range(2):
            bank = psum1.tile([NQ, PACK, P], F32, name=f"scores{h}")
            for j in range(PACK):
                nc.vector.scalar_tensor_tensor(
                    biased[:, h, j, :], raws[h][:, j, :], ts_cols[:, h, j : j + 1], bias[:, h, j, :], ALU.mult, ALU.add
                )
                nc.tensor.transpose(bank[:, j, :], biased[:, h, j, :], ident_f[:])
            banks.append(bank)

        negated = keep.tile([NQ, PACK, P], F32, name="negated")
        floors = keep.tile([NQ, 2], F32, name="floors")
        nc.vector.tensor_scalar(
            negated[:], banks[0][:], -1.0, None, ALU.mult, ALU.min, accum_out=floors[:, 0:1]
        )
        nc.vector.tensor_scalar(
            negated[:], banks[1][:], -1.0, floors[:, 0:1], ALU.mult, ALU.min, accum_out=floors[:, 1:2]
        )

        turn_values(3)
        quantize_values(1)

        probs = keep.tile([NQ, 2, PACK, P], F32, name="probs")
        sums = keep.tile([NQ, 3], F32, name="sums")
        for n, (h, j0, j1) in enumerate(((0, 0, 4), (1, 0, 2), (1, 2, 4))):
            nc.scalar.activation(
                probs[:, h, j0:j1],
                banks[h][:].rearrange("q b m -> q (b m)").rearrange("q (i j) -> q j i", j=PACK)[:, j0:j1],
                ACT.Exp,
                bias=floors[:, 1:2],
                accum_out=sums[:, n : n + 1],
            )
        w_codes = keep.tile([P, 2, NQ], U32, name="w_codes", align_bytes=64)
        w_scales = keep.tile([P, 2, NQ], U8, name="w_scales", align_bytes=64)
        weights = []
        for h in range(2):
            turned = psum2.tile([P, PACK, P], F32, name="turn")
            for t in range(PACK):
                nc.tensor.transpose(turned[:, t, :], probs[:, h, t, :], ident_f[:])
            w = keep.tile([P, NQ, PACK], BF16, name=f"w{h}", align_bytes=64)
            nc.vector.tensor_tensor(
                w[:],
                turned[:].rearrange("s t q -> s q t"),
                ts_spread[:, h, :].unsqueeze(1).to_broadcast([P, NQ, PACK]),
                ALU.mult,
            )
            weights.append(w)
        for h in range(2):
            nc.vector.quantize_mx(
                out=w_codes[:, h, :].bitcast(FP8X4), scales=w_scales[:, h, :], in_=weights[h][:].rearrange("s q t -> s (q t)")
            )
        total = keep.tile([P, 1], F32, name="total")
        nc.vector.reduce_sum(total[:], sums[:], axis=AX.X)
        inverse = keep.tile([P, 1], F32, name="inverse")
        nc.vector.reciprocal(inverse[:], total[:])

        outputs = []
        for v in range(2):
            y = psum1.tile([NQ, D // 2], F32, name=f"raw{v}")
            outputs.append(y)
        for h in range(2):
            for v in range(2):
                nc.tensor.matmul_mx(
                    out=outputs[v][:],
                    lhsT=w_codes[:, h, :].bitcast(FP8X4),
                    lhsT_scale=w_scales[:, h, :],
                    rhs=val_codes[:, h, v].rearrange("s t e -> s (t e)").bitcast(FP8X4),
                    rhs_scale=val_scales[:, h, v].rearrange("s t e -> s (t e)"),
                    start=(h == 0),
                    stop=(h == 1),
                )
        result = keep.tile([NQ, P, PACK], F32, name="result")
        ch_view = ch_sb[:].rearrange("q (e t) -> q e t", t=PACK)
        for v, queue in enumerate((nc.scalar, nc.sync)):
            part = slice(P // 2 * v, P // 2 * (v + 1))
            nc.vector.scalar_tensor_tensor(
                result[:, part],
                outputs[v][:].rearrange("q (t e) -> q e t", t=PACK),
                inverse[:],
                ch_view[:, part],
                ALU.mult,
                ALU.mult,
            )
            queue.dma_start(
                out=out[0][:, D // 2 * v : D // 2 * (v + 1)], in_=result[:, part].rearrange("q e t -> q (e t)")
            )
